import numpy as np
CORES = [96,97,98,99,100,101,102,103,112,113,114,115,116,117,118,119]
N = 16
def setup_inputs(rng):
    return {"x": rng.standard_normal((N, 128, 128), dtype=np.float32)}
def reference(x):
    s = x.sum(axis=0, dtype=np.float64).astype(x.dtype)
    b = 128 // N
    return {"y": np.stack([s[:, r * b:(r + 1) * b] for r in range(N)])}

@@ -1,0 +1,58 @@
+from concourse.bass import DstId, RemoteDMATransfer
+
+SCRATCH = {
+    "d": ("dram", [16, 128, 8], "float32"),
+    "land": ("dram", [16, 128, 8], "float32"),
+    "sq": ("dram", [512, 8], "float32"),
+}
+SEMAPHORES = ["ld", "a1", "a2", "snt", "st"]
+
+
+def rank_program(g, core, T, topo):
+    r = T.rank_of(core)
+    if r is None:
+        return
+    cores = T.cores
+    Q, P = divmod(r, 4)
+    mychip = topo.chip(core)
+
+    def dst_id(rank):
+        rid, pid, _se = topo.addr(cores[rank])
+        return DstId(rid=rid, pnc=pid)
+
+    far = [q for q in range(4) if topo.chip(cores[4 * q]) != mychip]
+    near = [q for q in range(4) if topo.chip(cores[4 * q]) == mychip]
+    for k, q in enumerate(far + near):
+        queue = g.sync if k % 2 == 0 else g.scalar
+        queue.dma_start(T.d[4 * q:4 * q + 4], T.x[:, 32 * q:32 * q + 32]).then_inc(T.sem.ld, 16)
+    g.wait_ge(T.sem.ld, 64)
+
+    transfers = []
+    e_far, e_near = 0, 8
+    for h in range(16):
+        if h == r:
+            continue
+        Qh, Ph = divmod(h, 4)
+        t = 4 * (Qh ^ 1) + Ph
+        if topo.chip(cores[h]) != mychip:
+            e = e_far
+            e_far += 1
+        else:
+            e = e_near
+            e_near += 1
+        transfers.append(RemoteDMATransfer(dst_ids=[dst_id(h)], dma_engine_mask=1 << e, remote_sem=T.sem.a1,
+                                           src=T.d[t], dst=T.land[r]))
+    g.remote_dma_fused(transfers, local_sem=T.sem.snt)
+    g.wait_ge(T.sem.a1, 15)
+
+    mine = 4 * (Q ^ 1) + P
+    srcs = [T.d[mine] if i == r else T.land[i] for i in range(16)]
+    outs = [4 * (Q ^ 1) + j for j in range(4)]
+    fold = RemoteDMATransfer(dst_ids=[dst_id(o) for o in outs], dma_engine_mask=0xFFFF, remote_sem=T.sem.a2,
+                             srcs=srcs, dsts=[T.sq[128 * P:128 * P + 128, :] for _o in outs], alu_op=1)
+    g.remote_dma_fused([fold], local_sem=T.sem.snt)
+
+    g.sync.wait_ge(T.sem.a2, 64)
+    g.sync.dma_start(T.y[:, :], T.sq[P::4, :]).then_inc(T.sem.st, 16)
+    g.sync.wait_ge(T.sem.st, 16)
+    g.wait_ge(T.sem.snt, 15 + 16)

@@ -5,7 +5,7 @@ SCRATCH = {
     "land": ("dram", [16, 128, 8], "float32"),
     "sq": ("dram", [512, 8], "float32"),
 }
-SEMAPHORES = ["ld", "a1", "a2", "snt", "st"]
+SEMAPHORES = ["ldf", "ldn", "a1", "a2", "snt", "st"]
 
 
 def rank_program(g, core, T, topo):
@@ -22,27 +22,26 @@ def rank_program(g, core, T, topo):
 
     far = [q for q in range(4) if topo.chip(cores[4 * q]) != mychip]
     near = [q for q in range(4) if topo.chip(cores[4 * q]) == mychip]
-    for k, q in enumerate(far + near):
-        queue = g.sync if k % 2 == 0 else g.scalar
-        queue.dma_start(T.d[4 * q:4 * q + 4], T.x[:, 32 * q:32 * q + 32]).then_inc(T.sem.ld, 16)
-    g.wait_ge(T.sem.ld, 64)
+    for group, sem in ((far, T.sem.ldf), (near, T.sem.ldn)):
+        for queue, q in zip((g.sync, g.scalar), group):
+            queue.dma_start(T.d[4 * q:4 * q + 4], T.x[:, 32 * q:32 * q + 32]).then_inc(sem, 16)
 
-    transfers = []
-    e_far, e_near = 0, 8
-    for h in range(16):
-        if h == r:
-            continue
-        Qh, Ph = divmod(h, 4)
-        t = 4 * (Qh ^ 1) + Ph
-        if topo.chip(cores[h]) != mychip:
-            e = e_far
-            e_far += 1
-        else:
-            e = e_near
-            e_near += 1
-        transfers.append(RemoteDMATransfer(dst_ids=[dst_id(h)], dma_engine_mask=1 << e, remote_sem=T.sem.a1,
-                                           src=T.d[t], dst=T.land[r]))
-    g.remote_dma_fused(transfers, local_sem=T.sem.snt)
+    def send(quarters, first_engine):
+        transfers = []
+        for q in quarters:
+            for p in range(4):
+                h = 4 * (q ^ 1) + p
+                if h == r:
+                    continue
+                transfers.append(RemoteDMATransfer(dst_ids=[dst_id(h)],
+                                                   dma_engine_mask=1 << (first_engine + len(transfers)),
+                                                   remote_sem=T.sem.a1, src=T.d[4 * q + p], dst=T.land[r]))
+        g.remote_dma_fused(transfers, local_sem=T.sem.snt)
+
+    g.wait_ge(T.sem.ldf, 32)
+    send(far, 0)
+    g.wait_ge(T.sem.ldn, 32)
+    send(near, 8)
     g.wait_ge(T.sem.a1, 15)
 
     mine = 4 * (Q ^ 1) + P

@@ -5,7 +5,7 @@ SCRATCH = {
     "land": ("dram", [16, 128, 8], "float32"),
     "sq": ("dram", [512, 8], "float32"),
 }
-SEMAPHORES = ["ldf", "ldn", "a1", "a2", "snt", "st"]
+SEMAPHORES = ["ld0", "ld1", "ld2", "ld3", "a1", "a2", "snt", "st"]
 
 
 def rank_program(g, core, T, topo):
@@ -21,28 +21,27 @@ def rank_program(g, core, T, topo):
         return DstId(rid=rid, pnc=pid)
 
     far = [q for q in range(4) if topo.chip(cores[4 * q]) != mychip]
-    near = [q for q in range(4) if topo.chip(cores[4 * q]) == mychip]
-    for group, sem in ((far, T.sem.ldf), (near, T.sem.ldn)):
-        for queue, q in zip((g.sync, g.scalar), group):
-            queue.dma_start(T.d[4 * q:4 * q + 4], T.x[:, 32 * q:32 * q + 32]).then_inc(sem, 16)
+    stages = [(far[0], 0, 2), (far[1], 0, 2), (Q, 8, 2), (Q ^ 1, 4, 4)]
 
-    def send(quarters, first_engine):
+    for k, (q, _e, _w) in enumerate(stages):
+        for half, queue in enumerate((g.sync, g.scalar)):
+            queue.dma_start(T.d[4 * q + 2 * half:4 * q + 2 * half + 2],
+                            T.x[64 * half:64 * half + 64, 32 * q:32 * q + 32]).then_inc(T.sem["ld%d" % k], 16)
+
+    sent = 0
+    for k, (q, first, width) in enumerate(stages):
         transfers = []
-        for q in quarters:
-            for p in range(4):
-                h = 4 * (q ^ 1) + p
-                if h == r:
-                    continue
-                transfers.append(RemoteDMATransfer(dst_ids=[dst_id(h)],
-                                                   dma_engine_mask=1 << (first_engine + len(transfers)),
-                                                   remote_sem=T.sem.a1, src=T.d[4 * q + p], dst=T.land[r]))
+        for p in range(4):
+            h = 4 * (q ^ 1) + p
+            if h == r:
+                continue
+            mask = ((1 << width) - 1) << (first + width * len(transfers))
+            transfers.append(RemoteDMATransfer(dst_ids=[dst_id(h)], dma_engine_mask=mask,
+                                               remote_sem=T.sem.a1, src=T.d[4 * q + p], dst=T.land[r]))
+            sent += width
+        g.wait_ge(T.sem["ld%d" % k], 32)
         g.remote_dma_fused(transfers, local_sem=T.sem.snt)
-
-    g.wait_ge(T.sem.ldf, 32)
-    send(far, 0)
-    g.wait_ge(T.sem.ldn, 32)
-    send(near, 8)
-    g.wait_ge(T.sem.a1, 15)
+    g.wait_ge(T.sem.a1, 16 + 8 + 12)
 
     mine = 4 * (Q ^ 1) + P
     srcs = [T.d[mine] if i == r else T.land[i] for i in range(16)]
@@ -54,4 +53,4 @@ def rank_program(g, core, T, topo):
     g.sync.wait_ge(T.sem.a2, 64)
     g.sync.dma_start(T.y[:, :], T.sq[P::4, :]).then_inc(T.sem.st, 16)
     g.sync.wait_ge(T.sem.st, 16)
-    g.wait_ge(T.sem.snt, 15 + 16)
+    g.wait_ge(T.sem.snt, sent + 16)

from concourse.bass import DstId, RemoteDMATransfer

SCRATCH = {
    "d": ("dram", [16, 128, 8], "float32"),
    "land": ("dram", [16, 128, 8], "float32"),
    "sq": ("dram", [512, 8], "float32"),
}
SEMAPHORES = ["ld0", "ld1", "ld2", "ld3", "a1", "a2", "snt", "st"]


def rank_program(g, core, T, topo):
    r = T.rank_of(core)
    if r is None:
        return
    cores = T.cores
    Q, P = divmod(r, 4)
    mychip = topo.chip(core)

    def dst_id(rank):
        rid, pid, _se = topo.addr(cores[rank])
        return DstId(rid=rid, pnc=pid)

    far = [q for q in range(4) if topo.chip(cores[4 * q]) != mychip]
    stages = [(far[0], 0, 2), (far[1], 0, 2), (Q, 8, 2), (Q ^ 1, 4, 4)]

    for k, (q, _e, _w) in enumerate(stages):
        for half, queue in enumerate((g.sync, g.scalar)):
            queue.dma_start(T.d[4 * q + 2 * half:4 * q + 2 * half + 2],
                            T.x[64 * half:64 * half + 64, 32 * q:32 * q + 32]).then_inc(T.sem["ld%d" % k], 16)

    sent = 0
    for k, (q, first, width) in enumerate(stages):
        transfers = []
        for p in range(4):
            h = 4 * (q ^ 1) + p
            if h == r:
                continue
            mask = ((1 << width) - 1) << (first + width * len(transfers))
            transfers.append(RemoteDMATransfer(dst_ids=[dst_id(h)], dma_engine_mask=mask,
                                               remote_sem=T.sem.a1, src=T.d[4 * q + p], dst=T.land[r]))
            sent += width
        g.wait_ge(T.sem["ld%d" % k], 32)
        g.remote_dma_fused(transfers, local_sem=T.sem.snt)
    g.wait_ge(T.sem.a1, 16 + 8 + 12)

    mine = 4 * (Q ^ 1) + P
    srcs = [T.d[mine] if i == r else T.land[i] for i in range(16)]
    outs = [4 * (Q ^ 1) + j for j in range(4)]
    fold = RemoteDMATransfer(dst_ids=[dst_id(o) for o in outs], dma_engine_mask=0xFFFF, remote_sem=T.sem.a2,
                             srcs=srcs, dsts=[T.sq[128 * P:128 * P + 128, :] for _o in outs], alu_op=1)
    g.remote_dma_fused([fold], local_sem=T.sem.snt)

    g.sync.wait_ge(T.sem.a2, 64)
    g.sync.dma_start(T.y[:, :], T.sq[P::4, :]).then_inc(T.sem.st, 16)
    g.sync.wait_ge(T.sem.st, 16)
    g.wait_ge(T.sem.snt, sent + 16)
